import numpy as np, ml_dtypes
CORES = [40,41,42,43,44,45,46,47]
N = 8
BF = ml_dtypes.bfloat16
def gentries(a):
    return np.ascontiguousarray(a.reshape(8, 16, -1).transpose(0, 2, 1)).reshape(8, -1)
def gtable(e):
    e = np.asarray(e); return np.ascontiguousarray(e.reshape(8, -1, 16).transpose(0, 2, 1)).reshape(128, -1).astype(np.int32)
R0, I0, B0, F, CAP, RO = 512, 2048, 4096, 2048, 272, 2
def weigh(b):
    return np.add.reduce(b * (2 * np.arange(16) + 1)[:, None], axis=-2)
def parts(rng):
    return (rng.integers(0, I0, (N, 8, 16, R0)), rng.integers(0, B0, (N, 8, 16, I0)), rng.integers(0, 256, (N, 8, 16, B0)), rng.integers(0, R0, (N, 8, F)), rng.integers(0, 256, (N, 8, F)))
def pack(rc, ic, b, cur, x):
    return {"rtab": np.ascontiguousarray(rc.reshape(N, 128, R0)).astype(np.int32), "itab": np.ascontiguousarray(ic.reshape(N, 128, I0)).astype(np.int32),
            "btab": np.ascontiguousarray(b.reshape(N, 128, B0)).astype(np.float32).astype(BF), "rn0": np.stack([gtable(a) for a in cur]), "x0": np.ascontiguousarray(x).astype(np.int32)}
def heavy(rng, w):
    b = rng.integers(0, 16, w.shape[:-1] + (16,) + w.shape[-1:]); b = np.where((weigh(b) > w)[..., None, :], 0, b); rest = w - weigh(b)
    for i in range(15, -1, -1):
        a = np.minimum(255 - b[..., i, :], rest // (2 * i + 1)); b[..., i, :] += a; rest = rest - a * (2 * i + 1)
    return b
def setup_inputs(rng):
    return pack(*parts(rng))
def setup_inputs_room(rng):
    rc, ic, b, cur, x = parts(rng)
    w = weigh(b) - b[:, :, 0]; b[:, :, 0] = b[:, :, 0] // N * N + ((np.arange(B0) - w) & (N - 1))
    ic = ic // N * N + (np.arange(16) & (N - 1))[:, None]
    for a in range(N):
        for g in range(8):
            n = int(rng.choice(np.array([0, 1, CAP - 1, CAP, CAP + 1, 2 * CAP, F]))); m = int(rng.integers(0, N))
            if a == 0: m = 1; n = (CAP, CAP + 1, F, CAP - 1, 1, 0, CAP, 2 * CAP)[g]
            e = rng.permutation(np.concatenate([np.full(n, m), (m + rng.integers(1, N, F - n)) & (N - 1)]))
            d2 = ((e - np.arange(F)) & (N - 1)) + N * rng.integers(0, 16 // N, F)
            x[a, g] = (x[a, g] & 15) + 16 * d2
    return pack(rc, ic, b, cur, x)
def setup_inputs_full(rng):
    rc, ic, b, cur, x = parts(rng); m = int(rng.integers(0, N)); P = 1 << (B0 - 1).bit_length(); f = np.arange(F); k = np.arange(N); n = CAP // N
    for g in range(8):
        col = np.argsort(rng.random((N, B0 // N)), axis=1)[:, :CAP] * N + k[:, None]
        for a in range(N):
            late = np.argsort(rng.random((N, F // 2 // N)), axis=1)[:, :n] * N + k[:, None] + F // 2
            e = (m + rng.integers(1, N, F)) & (N - 1); w = ((e - f) & (N - 1)) + N * rng.integers(0, 65280 // N, F)
            c = col[(m - k) & (N - 1), a * n:(a + 1) * n]; w[late] = c + P * rng.integers(0, (65280 - c) // P + 1)
            q = rng.permutation(16 * R0)[:F]; inn = rng.permutation(I0)[:F]; blk = rng.permutation(B0)[:F]; d2 = rng.integers(0, 16, F)
            rc[a, g, q // R0, q % R0] = inn; ic[a, g, d2, inn] = blk; b[a, g][:, blk] = heavy(rng, w)
            cur[a, g] = q % R0; x[a, g] = q // R0 + 16 * d2
    return pack(rc, ic, b, cur, x)
def setup_inputs_deep(rng):
    rc, ic, b, cur, x = parts(rng)
    e = np.array([7, 6, 5, 4, 7, 6, 4, 3])[:, None, None]
    b = (b >> e) << e; x = (x >> e[:, :, 0]) << e[:, :, 0]
    b[:, 4:, 0] += 1; x[:, 4:] += 4
    return pack(rc, ic, b, cur, x)
def setup_inputs_ends(rng):
    rc, ic, b, cur, x = parts(rng); tg = [0, 1, 7, 8, 65279, 65280]; h = N // 2
    for t in range(RO):
        c = B0 + t * F; p = 1 << (c - 1).bit_length(); tg += [c - 1, c, c + 1, p - 1, p, p + c]
    b[::2, ::2] = heavy(rng, rng.choice(np.array(tg), (h, 4, B0)))
    b[::2, 1::4] = 255 * (b[::2, 1::4] & 1)
    rc[::2, 7] = (I0 - 1) * rng.integers(0, 2, (h, 16, R0)); ic[::2, 7] = (B0 - 1) * rng.integers(0, 2, (h, 16, I0)); cur[::2, 7] = (R0 - 1) * rng.integers(0, 2, (h, F))
    b[::2, 3] = np.where(rng.random((h, 1, B0)) < 0.25, 0, b[::2, 3]); b[:, 3, :, 0] = ((256 - RO) * 171) & 255
    cur[1::2, 0:6:2] = rng.integers(0, R0, (h, 3, 1)); rc[1::2, 1::4] = rng.integers(0, I0, (h, 2, 1, R0)); ic[1::2, 3] = rng.integers(0, B0, (h, 1, I0))
    b[1::2, 2] = np.take_along_axis(b[1::2, 2, :, :3], rng.integers(0, 3, (h, 1, B0)), 2)
    x[1::2, 4:6] = rng.integers(0, 256, (h, 2, 1))
    for g, z in ((6, 0), (7, int(rng.integers(1, 8)))):
        e = rng.integers(0, 256, 16); n = rng.integers(0, 256, 16)
        rest = int(weigh(n[:, None])[0]) - int(n[0]); n[0] = int(n[0]) // 8 * 8 + ((z - rest) & 7)
        old = (n - 3 * e) & 255; key = int(weigh(n[:, None])[0]) & 255
        v = int(weigh(old[:, None])[0]) & ((1 << (B0 - 1).bit_length()) - 1)
        if v >= B0: v -= B0
        c = (v + 1) % B0
        b[:, g, :, v] = e; b[1::2, g, :, c] = old; ic[1::2, g, key >> 4] = c; x[1::2, g] = key
    return pack(rc, ic, b, cur, x)
def setup_inputs_spread(rng):
    rc, ic, b, cur, x = parts(rng); k = rng.choice(np.array([1.0, 3.0, 8.0]), (N, 8, 1, 1))
    rc = np.minimum((I0 * rng.random((N, 8, 16, R0)) ** k).astype(np.int64), I0 - 1)
    ic = np.minimum((B0 * rng.random((N, 8, 16, I0)) ** k).astype(np.int64), B0 - 1)
    cur = np.minimum((R0 * rng.random((N, 8, F)) ** k[..., 0]).astype(np.int64), R0 - 1)
    b = b >> rng.integers(0, 9, (N, 8, 1, B0)); x = x >> rng.integers(0, 9, (N, 8, F))
    return pack(rc, ic, b, cur, x)
def check_inputs(d):
    bad = []
    for k, hi in (("rtab", I0 - 1), ("itab", B0 - 1), ("rn0", R0 - 1), ("x0", 255)):
        if np.min(d[k]) < 0 or np.max(d[k]) > hi: bad.append("range of " + k)
    v = np.asarray(d["btab"]).astype(np.float32)
    if not np.all((v >= 0) & (v <= 255) & (v == np.floor(v))): bad.append("whole numbers of btab")
    return bad
def reference(rtab, itab, btab, rn0, x0):
    r = rtab.astype(np.int64).reshape(N, 8, 16, R0); s = itab.astype(np.int64).reshape(N, 8, 16, I0); b = btab.astype(np.float32).astype(np.int64).reshape(N, 8, 16, B0)
    cur = np.stack([gentries(a) for a in rn0]).astype(np.int64); x = x0.astype(np.int64)
    f = np.arange(F); row = np.arange(16)[:, None]
    for t in range(RO):
        C = B0 + t * F; P = 1 << (C - 1).bit_length()
        d1 = (x & 15)[:, :, None, :]; d2 = ((x >> 4) & 15)[:, :, None, :]
        rc = np.take_along_axis(r, cur[:, :, None, :], 3)
        ic = np.take_along_axis(s, np.take_along_axis(rc, d1, 2), 3)
        old = np.take_along_axis(b, np.take_along_axis(ic, d2, 2), 3)
        h = weigh(old)
        to = (h + f) & (N - 1); v = h & (P - 1); v = np.where(v >= C, v - C, v)
        ok = np.zeros(to.shape, bool)
        for q in range(N):
            m = (to == q).astype(np.int64)
            ok |= (m == 1) & (np.add.accumulate(m, axis=2) - m < CAP)
        far = b[to[:, :, None, :], np.arange(8)[:, None, None], row, v[:, :, None, :]]
        far = np.where(ok[:, :, None, :], far, 0)
        new = (old + 3 * far + t) & 255
        ic = np.where(row == d2, B0 + t * F + f, ic); rc = np.where(row == d1, I0 + t * F + f, rc)
        b = np.concatenate([b, new], axis=3); s = np.concatenate([s, ic], axis=3); r = np.concatenate([r, rc], axis=3)
        x = weigh(new)
        cur = R0 + t * F + np.where((x & 7) == 0, (x >> 3) & (F - 1), f)
    return {"yb": new.reshape(N, 128, F).astype(np.float32).astype(BF), "yi": ic.reshape(N, 128, F).astype(np.float32), "yn": cur.astype(np.float32)}

from concourse.bass import DstId, RemoteDMATransfer
from concourse.mybir import AluOpType, ActivationFunctionType

N, F, CAP = 8, 2048, 272
LC = CAP // 16
SLOTS = N * CAP
NC_SEM, ND_SEM = 100, 30
OPT = {"split_rq": True, "split_rp": True, "act_new": (2, 3), "hyb": 60}
ORDER = [16,8,11,13,9,0,4,1,15,14,17,10,21,6,19,30,20,25,34,23,28,2,67,24,31,37,38,68,26,78,3,27,69,71,79,22,70,84,5,76,73,89,86,82,85,90,83,35,75,87,77,39,74,88,81,33,80,91,92,7,93,45,94,97,98,95,96,29,101,102,99,100,40,36,49,103,41,104,105,12,44,43,55,18,54,106,107,63,108,62,42,112,51,113,149,32,114,48,109,116,66,50,110,57,72,115,117,111,119,120,64,118,122,121,65,123,125,124,146,169,147,156,144,47,126,127,150,128,151,129,130,131,132,162,157,165,167,166,143,135,153,148,164,46,161,163,133,152,159,136,58,158,145,137,139,154,155,138,168,140,142,134,141,173,179,170,174,182,176,183,177,175,180,185,178,186,191,192,60,184,193,196,197,194,199,181,198,216,195,200,217,218,201,221,205,219,222,220,223,187,224,202,207,230,225,204,226,227,53,206,189,203,232,208,190,209,229,233,210,211,228,231,234,212,235,188,236,213,214,237,238,215,241,239,248,172,242,240,245,243,56,244,246,247,252,253,254,298,256,299,160,250,255,171,257,251,52,259,258,260,282,262,249,281,263,261,264,265,295,283,266,296,267,268,269,288,286,285,271,287,289,291,270,297,294,302,272,284,276,278,275,308,279,277,290,303,280,304,305,273,274,292,309,293,312,300,59,61,301,306,307,315,313,324,310,318,319,316,321,314,322,329,320,335,317,323,332,325,326,327,311,328,331,334,330,338,337,340,341,342,333,343,339,344,345,346,336,347,348]
SWAP = [101,102,139,173,176,179,182,241,242,274,307,315,318]

BF, F32, I32, U16 = "bfloat16", "float32", "int32", "uint16"
SCRATCH = {"psv": ("psum", [128, 2048], F32), "psc": ("psum", [128, 1024], F32), "psl": ("psum", [128, 1024], F32),
           "pp": ("sbuf", [128, 2048], "float16"), "zo": ("sbuf", [128, 144], "float16")}
for _d, _w, _names in (
        (I32, 128, "rns xb ti0 ti1 ti2 ti3 ti4"), (I32, 512, "rt"), (I32, 2048, "itr"), (I32, 136, "lz lv"), (I32, 4, "pi"),
        (U16, 128, "rnu xu inu bku su spu rpu"), (U16, 144, "rqo0 rqo1"), (U16, 120, "rqi0 rqi1"),
        (F32, 4096, "wi"), (F32, 2048, "r0 hrow frow"), (F32, 8192, "wina"), (F32, 136, "lsa zer"), (F32, 1024, "mx"),
        (F32, 256, "e1f e2f sa sb so"), (F32, 12, "col"), (F32, 160, "nrow"), (F32, 128, "f8a f8b fyb tf0 tf1 tf2 tf3 tf4"),
        (BF, 8192, "wb"), (BF, 16384, "winb"), (BF, 2048, "m1 m2 old far qq"), (BF, 1904, "sv0 sv1"), (BF, 2184, "land0 land1"),
        (BF, 1024, "oh scn"), (BF, 512, "rst qpat ones"), (BF, 256, "e1 e2"), (BF, 144, "zw zw3 zwn"), (BF, 160, "zh0 zh1"),
        (BF, 128, "xtb xtt pq wrow blk tri idb id3 idn cs0 cs1 cr ci tob")):
    for _n in _names.split():
        SCRATCH[_n] = ("sbuf", [128, _w], _d)

SEMAPHORES = (["c%d" % k for k in range(NC_SEM)] + ["d%d" % k for k in range(ND_SEM)]
              + ["rq00", "rq01", "rq10", "rq11", "rp0", "rp1", "lf0", "lf1", "lf2", "lf3"])

ALU = AluOpType
ACT = ActivationFunctionType


def touch(o, e):
    for (b, lo, hi) in o["w"]:
        for (b2, lo2, hi2) in e["w"] + e["r"]:
            if b == b2 and lo < hi2 and lo2 < hi: return True
    for (b, lo, hi) in o["r"]:
        for (b2, lo2, hi2) in e["w"]:
            if b == b2 and lo < hi2 and lo2 < hi: return True
    return False


def emit(g, T, steps):
    order = ORDER if ORDER else list(range(len(steps)))
    pos = {s: n for n, s in enumerate(order)}
    ops = []
    for s in order:
        o = dict(steps[s])
        if s in SWAP: o["q"], o["fn"] = o["alt"]
        o["after"] = [pos[m] for m in o["after"]]
        ops.append(o)
    eng = {"V": g.vector, "A": g.scalar, "P": g.tensor, "S": g.sync, "G": g}
    known = {q: 0 for q in eng}
    at, waits, needed = [], [], set()
    for n, o in enumerate(ops):
        deps = set(o["after"])
        for m in range(n):
            e = ops[m]
            if (e["q"] != o["q"] and (o["banks"] & e["banks"])) or touch(o, e): deps.add(m)
        mine = []
        for m in sorted(deps, reverse=True):
            if not (known[o["q"]] >> m) & 1:
                mine.append(m); needed.add(m)
                known[o["q"]] |= (1 << m) | at[m]
        at.append(known[o["q"]]); waits.append(mine)
    last, count, sig, seen = {}, {}, {}, set()
    for n, o in enumerate(ops):
        q = eng[o["q"]]
        for m in waits[n]:
            q.wait_ge(T.sem[sig[m][0]], sig[m][1])
        for (s, v) in o["ext"]:
            if (o["q"], s, v) not in seen:
                seen.add((o["q"], s, v)); q.wait_ge(T.sem[s], v)
        s = None
        if n in needed:
            pool = ["d%d" % k for k in range(ND_SEM)] if o["dma"] else ["c%d" % k for k in range(NC_SEM)]
            s = [p for p in pool if p not in last or (at[n] >> last[p]) & 1][0]
            last[s] = n
        for fn in o["fn"]:
            ins = fn()
            if s is not None:
                inc = 16 if o["dma"] else 1
                ins.then_inc(T.sem[s], inc); count[s] = count.get(s, 0) + inc
        if s is not None: sig[n] = (s, count[s])


def rank_program(g, core, T, topo):
    if T.rank_of(core) is not None:
        emit(g, T, steps_of(g, core, T, topo))


def steps_of(g, core, T, topo):
    me = T.rank_of(core)
    ops = []
    V, A, P, S = g.vector, g.scalar, g.tensor, g.sync
    bank0 = {"psv": 0, "psc": 4, "psl": 6}

    def R(b, lo=0, hi=None, st=1):
        hi = T[b].shape[1] if hi is None else hi
        return (T[b][:, lo:hi] if st == 1 else T[b][:, lo:hi:st], (b, lo, hi))

    def IND(win, off):
        return (win[0].indirect(off[0]), win[1], off[1])

    def add(q, fn, r, w, ext=(), dma=False, after=(), alt=None, sends=()):
        banks, rr, ww = set(), [], []
        for src, dst in ((r, rr), (w, ww)):
            for x in src:
                for (b, lo, hi) in x[1:]:
                    if b in bank0: banks |= set(range(bank0[b] + lo // 512, bank0[b] + (hi - 1) // 512 + 1))
                    else: dst.append((b, lo, hi))
        ops.append({"q": q, "fn": fn, "r": rr, "w": ww, "banks": banks, "ext": list(ext), "dma": dma, "after": list(after),
                    "alt": alt, "sends": list(sends)})
        return len(ops) - 1

    def aps(xs):
        return [x for x in xs if isinstance(x, tuple)]

    def val(x):
        return x[0] if isinstance(x, tuple) else x

    def ts_(o, i, s1, s2, op0, op1=None):
        if op1 is None: return lambda: V.tensor_scalar(o[0], i[0], val(s1), None, op0)
        return lambda: V.tensor_scalar(o[0], i[0], val(s1), val(s2), op0, op1)

    def ts(o, i, s1, op0, s2=None, op1=None):
        return add("V", [ts_(o, i, s1, s2, op0, op1)], [i] + aps([s1, s2]), [o])

    def tt(o, a, b, op):
        return add("V", [lambda: V.tensor_tensor(o[0], a[0], b[0], op)], [a, b], [o])

    def scan(o, a, b, op1):
        return add("V", [lambda: V.tensor_tensor_scan(o[0], a[0], b[0], 0.0, ALU.mult, op1)], [a, b], [o])

    def cp(o, i):
        return add("V", [lambda: V.tensor_copy(o[0], i[0])], [i], [o])

    def act(o, i, func, scale=1.0, bias=0.0):
        return add("A", [lambda: A.activation(o[0], i[0], func, bias=bias, scale=scale)], [i], [o])

    def either(q, o, i, bias=0.0, ext=()):
        if bias == 0.0:
            fn = {"V": lambda: V.tensor_copy(o[0], i[0]), "A": lambda: A.activation(o[0], i[0], ACT.Identity)}
        else:
            fn = {"V": ts_(o, i, bias, None, ALU.add), "A": lambda: A.activation(o[0], i[0], ACT.Identity, bias=bias)}
        x = "A" if q == "V" else "V"
        return add(q, [fn[q]], [i], [o], ext, alt=(x, [fn[x]]))

    def gat(q, o, win, off, ext=()):
        return either(q, o, IND(win, off), 0.0, ext)

    def mm(items):
        fns = [(lambda o=o, l=l, r=r, a=a, z=z: P.matmul(o[0], l[0], r[0], a, z)) for (o, l, r, a, z) in items]
        return add("P", fns, [x for it in items for x in it[1:3]], [it[0] for it in items])

    def dma(q, o, i, r, w, ext=(), after=()):
        return add(q, [lambda: (S if q == "S" else A).dma_start(o, i)], r, w, ext, True, after)

    def iota(o, pat, base, ch, flt=True):
        if flt: return add("G", [lambda: g.iota(o[0], pat, base, ch, allow_small_or_imprecise_dtypes=True)], [], [o])
        return add("G", [lambda: g.iota(o[0], pat, base, ch)], [], [o])

    def sel(o, i, pat, op, fill, base, ch):
        return add("G", [lambda: g.affine_select(o[0], i[0], pat, op, fill, base, ch)], [i], [o])

    def mset(o, c):
        return add("V", [lambda: V.memset(o[0], c)], [], [o])

    def lps(h):
        return R("psl", 448 + 64 * h, 512 + 64 * h)

    def to_list(z, src, h, start=True, stop=True, const=None):
        it = [] if const is None else [(lps(h), R(const), R("ones", 0, 64), True, False)]
        mm(it + [(lps(h), R(z, 15 - j, 143 - j), R(src, 1024 * h + j, 1024 * h + 1024, 16), start and j == 0 and const is None, stop and j == 15)
                 for j in range(16)])

    def H(b, h): return R(b, 64 * h, 64 * h + 64)
    def HR(b, h, base=0): return R(b, base + 1024 * h, base + 1024 * h + 1024)
    def CL(b, k): return R(b, 32 * k, 32 * k + 32)
    def CR(b, k, base=0): return R(b, base + 512 * k, base + 512 * k + 512)
    def col(k): return R("col", k, k + 1)

    dma("S", T.xb[:], T.x0[:], [], [R("xb")])
    dma("A", T.rns[:], T.rn0[:], [], [R("rns")])
    dma("S", T.rt[:], T.rtab[:], [], [R("rt")])
    for k in range(4):
        dma("S", CR("itr", k)[0], T.itab[:, 512 * k:512 * k + 512], [], [CR("itr", k)])
    ld = dma("S", T.wb[:, 0:4096], T.btab[:], [], [R("wb", 0, 4096)])

    iota(R("pi", 0, 1), [[0, 1]], 0, 1, False)
    iota(R("nrow"), [[1, 160]], 0, 0)
    iota(R("e1f"), [[0, 16], [1, 16]], 0, 0)
    iota(R("e2f"), [[1, 16], [0, 16]], 0, 0)
    mset(R("zer"), 0.0)
    ts(R("pi", 1, 2), R("pi", 0, 1), 15, ALU.bitwise_and)
    ts(R("pi", 2, 3), R("pi", 0, 1), 7, ALU.bitwise_and)
    ts(R("pi", 3, 4), R("pi", 0, 1), 4, ALU.arith_shift_right, 1, ALU.bitwise_and)
    mset(R("ones"), 1.0)
    cp(R("col", 0, 4), R("pi", 0, 4))
    mset(R("cr"), -16.0)
    ts(col(4), col(0), 16.0, ALU.add)
    ts(col(5), col(3), -1.0, ALU.mult, 1.0, ALU.add)
    tt(col(6), col(0), col(1), ALU.subtract)
    ts(col(8), col(1), 2.0, ALU.mult, 1.0, ALU.add)
    ts(R("zh1"), R("nrow"), col(4), ALU.is_equal, col(3), ALU.mult)
    ts(R("zh0"), R("nrow"), col(4), ALU.is_equal, col(5), ALU.mult)
    ts(col(7), col(6), 15.0, ALU.add)
    ts(R("e1f"), R("e1f"), col(1), ALU.is_equal, 4096.0, ALU.mult)
    act(R("e1"), R("e1f"), ACT.Silu)
    ts(R("zo"), R("nrow", 0, 144), col(7), ALU.is_equal)
    ts(R("zw"), R("nrow", 0, 144), col(7), ALU.is_equal, col(8), ALU.mult)
    ts(R("e2f"), R("e2f"), col(1), ALU.is_equal, 10240.0, ALU.mult)
    either("A", R("e2"), R("e2f"), -2048.0)
    GP, GN = [[-16, 8], [0, 16]], [[16, 8], [0, 16]]
    sel(R("idb"), R("ones", 0, 128), [[-1, 128]], ALU.is_equal, 0.0, 0, 1)
    iota(R("qpat"), [[0, 64], [1, 8]], 0, 0)
    iota(R("wrow"), [[-32, 8], [0, 16]], 1, 2)
    sel(R("wrow"), R("wrow"), GP, ALU.is_ge, 0.0, 0, 1)
    sel(R("wrow"), R("wrow"), GN, ALU.is_ge, 0.0, 15, -1)
    iota(R("tri"), [[0, 128]], -1, 0)
    sel(R("tri"), R("tri"), [[-1, 128]], ALU.is_gt, 0.0, 0, 1)
    sel(R("tri"), R("tri"), GN, ALU.is_ge, 0.0, 15, -1)
    sel(R("tri"), R("tri"), [[-1, 128]], ALU.not_equal, 4096.0, 0, 1)
    iota(R("f8a"), [[128, 128]], 0, 8)
    iota(R("f8b"), [[8, 128]], 0, 1024)
    iota(R("frow"), [[1, 2048]], 2048, 0)
    act(R("blk"), R("wrow"), ACT.Sign)
    act(R("rst"), R("qpat"), ACT.Sign)
    act(R("id3"), R("idb"), ACT.Identity, 3.0)
    act(R("idn"), R("idb"), ACT.Identity, -1.0)
    act(R("zw3"), R("zw"), ACT.Identity, 3.0)
    act(R("zwn"), R("zw"), ACT.Identity, -1.0)
    for t in range(2):
        c = T["cs%d" % t]
        add("V", [lambda c=c: V.memset(c[0:64, :], 768.0), lambda c=c, t=t: V.memset(c[64:96, :], t / 32.0),
                  lambda c=c: V.memset(c[96:128, :], 0.0)], [], [R("cs%d" % t)])
        mset(R("land%d" % t, SLOTS, SLOTS + 8), 0.0)
    mset(R("ci"), 224.0)
    ts(col(9), col(6), -8.0, ALU.mult)
    ts(col(10), col(6), -1024.0, ALU.mult)
    mset(R("sa"), 0.0)
    ts(R("f8a"), R("f8a"), col(9), ALU.add)
    ts(R("f8b"), R("f8b"), col(10), ALU.add)
    ts(R("sb", 1, 256, 2), R("f8a"), 0.125, ALU.mult)
    ts(R("fyb"), R("f8b"), 0.125, ALU.mult, 2560.0, ALU.add)
    for h in range(2):
        either("A", HR("frow", h), HR("frow", h), 2.0 ** -12)

    def zero_windows(ext=()):
        dma("S", T.wina[0:128:16, 0:SLOTS], T.zer[:], [R("zer")], [R("wina")], ext)
        iota(R("winb", 0, SLOTS), [[0, SLOTS]], 0, 0)
    zero_windows()
    ld = dma("S", T.wb[:, 6144:8192], T.btab[:, 0:2048], [], [R("wb", 6144, 8192)], after=[ld])

    cp(R("xtb"), R("xb"))
    add("V", [lambda: V.transpose(T.xtt[:], T.xtb[:])], [R("xtb")], [R("xtt")])
    mm([(R("psl", 2 * b + al, 128, 8), R("zh%d" % al, 16 - 16 * (gl - al), 144 - 16 * (gl - al)), R("xtt", 32 * b + 16 * gl, 32 * b + 16 * gl + 16),
         gl == 0, gl == 1) for b in range(4) for al in range(2) for gl in range(2)])
    cp(R("rnu"), R("rns"))
    cp(R("xu"), R("psl", 0, 128))

    def count_start():
        mm([(CR("psc", b), R("idb"), R("qpat"), True, False) for b in range(2)])

    count_start()
    for k in range(4):
        gat("A", CR("m1", k), R("e1"), CL("xu", k))
        gat("A", CR("m2", k), R("e2"), CL("xu", k))
        ts(CR("wi", k), CR("itr", k), -2048.0, ALU.add)
    for h in range(2):
        for k in (2 * h, 2 * h + 1):
            tt(CR("pp", k), IND(R("rt"), CL("rnu", k)), CR("m1", k), ALU.min)
        to_list("zo", "pp", h)
        cp(H("inu", h), lps(h))
    for h in range(2):
        for k in (2 * h, 2 * h + 1):
            tt(CR("pp", k), IND(R("wi", 0, 2048), CL("inu", k)), CR("m2", k), ALU.min)
        to_list("zo", "pp", h)
        ts(H("bku", h), lps(h), 32768.0, ALU.add)

    def old_blocks(win):
        for h in range(2):
            for k in (2 * h, 2 * h + 1):
                gat("AV"[k & 1], CR("old", k), win, CL("bku", k))
            to_list("zw", "old", h)
    old_blocks(R("wb", 0, 4096))

    place = {r: n for n, r in enumerate(sorted(range(N), key=lambda r: (topo.die(T.cores[r]), r)))}
    WAVE = ((4, 5, 1, 2), (6, 7, 3))
    order = [[s for s in range(N) if place[s] == place[me] ^ x][0] for w in WAVE for x in w]
    left = {}

    def send(slots, split, src, dst, sem, lf, r):
        trs, seen = [], {True: 0, False: 0}
        n = 4 if split else 2
        for k in slots:
            q = order[k]; other = topo.die(T.cores[q]) != topo.die(core)
            rid, pid, _ = topo.addr(T.cores[q])
            m = 0
            for x in topo.engines(core, T.cores[q])[(0 if other else 1)::2][n * seen[other]:n * seen[other] + n]: m |= 1 << x
            trs.append(RemoteDMATransfer(dst_ids=[DstId(rid=rid, pnc=pid)], dma_engine_mask=m, remote_sem=T.sem[sem], src=src(k), dst=dst(k)))
            seen[other] += 1
        left[lf] = left.get(lf, 0) + n * len(slots)
        return add("G", [lambda: g.remote_dma_fused(trs, local_sem=T.sem[lf])], r, [], sends=[sem, lf])
    n_rp = (4 if OPT["split_rp"] else 2) * (N - 1)

    def exchange(t, idle):
        rqo, rqi, sv, land = "rqo%d" % t, "rqi%d" % t, "sv%d" % t, "land%d" % t
        win = R("wb", 0, 4096 if t == 0 else 8192)
        ts(R("ti0"), R("psl", 448, 576), col(2), ALU.add)
        for k in range(2):
            mm([(CR("psv", k), R("wrow"), CR("old", k), True, True)])
            either("A", CR("hrow", k), CR("psv", k), 8192.0)
        ts(R("ti1"), R("ti0"), 7, ALU.bitwise_and)
        cp(R("tob"), R("ti1"))
        add("V", [ts_(R("oh", q, 1024, 8), R("tob"), float(q), 8.0, ALU.is_equal, ALU.mult) for q in range(N)], [R("tob")], [R("oh")])
        mm([(CR("psc", b), R("tri"), CR("oh", b), False, False) for b in range(2)])
        add("V", [(lambda q=q: V.tensor_tensor_scan(T.scn[:, q:1024:8], T.ones[:, 0:128], T.oh[:, q:1024:8], 0.0, ALU.mult, ALU.add))
                  for q in range(N)], [R("oh"), R("ones")], [R("scn")])
        for b in range(2):
            mm([(CR("psc", b), R("blk"), CR("scn", b), False, True)])
        ca = OPT["hyb"]
        oa = (T.wina[:].indirect(T.spu[:, 0:ca]), R("wina")[1])
        ob = (T.winb[:].indirect(T.spu[:, ca:128]), R("winb")[1])
        scan(CR("mx", 0), R("rst"), CR("psc", 0), ALU.max)
        ts(R("spu", 0, ca), R("mx", 7, 8 * ca, 8), -32776.0, ALU.add)
        add("A", [lambda: A.activation(oa[0], T.hrow[:, 0:16 * ca], ACT.Silu)], [R("hrow", 0, 16 * ca), R("spu", 0, ca)], [oa])
        scan(CR("mx", 1), R("rst"), CR("psc", 1), ALU.max)
        ts(R("spu", ca, 128), R("mx", 8 * ca + 7, 1024, 8), -32776.0, ALU.add)
        add("V", [lambda: V.tensor_copy(ob[0], T.old[:, 16 * ca:2048])], [R("old", 16 * ca, 2048), R("spu", ca, 128)], [ob])
        dma("A", T.lsa[:], T.wina[0:128:16, 0:SLOTS], [R("wina")], [R("lsa")], after=[ld])
        mm([(R("psc", 0, 136), R("zw", 15 - j, 143 - j), R("winb", 136 * j, 136 * j + 136), j == 0, j == 15) for j in range(16)])
        tt(R("lz"), R("psc", 0, 136), R("lsa"), ALU.add)
        ts(R("lv"), R("lz"), 4095 if t == 0 else 8191, ALU.bitwise_and)

        def pick(ks):
            add("V", [(lambda k=k: V.tensor_copy(T[rqo][:, 18 * k:18 * k + LC], T.lv[:, (order + [me])[k]:136:8])) for k in ks],
                [R("lv")], [R(rqo, 18 * ks[0], 18 * ks[-1] + 18)])

        def ask(ks, split, sem):
            send(ks, split, lambda k: T[rqo][:, 18 * k:18 * k + LC], lambda k: T[rqi][:, LC * k:LC * k + LC], sem, "lf%d" % (2 * t),
                 [R(rqo, 18 * ks[0], 18 * ks[-1] + 18)])
        if OPT["split_rq"]:
            pick([0, 1, 2, 3]); ask([0, 1, 2, 3], True, "rq%d0" % t)
            pick([4, 5, 6]); ask([4, 5, 6], True, "rq%d1" % t)
            ext = [[("rq%d0" % t, 16)], [("rq%d1" % t, 12)]]
        else:
            pick(list(range(7))); ask(list(range(7)), False, "rq%d0" % t)
            ext = [[("rq%d0" % t, 14)]] * 2
        pick([7])
        gat("A", R(land, CAP * me, CAP * me + CAP), win, R(rqo, 18 * 7, 18 * 7 + LC))

        def serve(q, a, b, e):
            gat(q, R(sv, a * CAP, b * CAP), win, R(rqi, a * LC, b * LC), e)

        def reply(ks, split):
            send(ks, split, lambda k: T[sv][:, CAP * k:CAP * k + CAP], lambda k: T[land][:, CAP * me:CAP * me + CAP], "rp%d" % t, "lf%d" % (2 * t + 1),
                 [R(sv, CAP * ks[0], CAP * ks[-1] + CAP)])
        if OPT["split_rp"]:
            serve("V", 0, 2, ext[0]); serve("A", 2, 4, ext[0]); reply([0, 1, 2, 3], True)
            serve("A", 4, 6, ext[1]); serve("V", 6, 7, ext[1]); reply([4, 5, 6], True)
        else:
            serve("V", 4, 7, ext[1]); serve("A", 0, 4, ext[0]); reply(list(range(7)), False)
        if t == 0: zero_windows([("lf1", left["lf1"])])
        for k in range(4):
            mm([(CR("psv", k), R("cs%d" % t), R("ones"), True, False), (CR("psv", k), R("idb"), CR("old", k), False, False)])
        sp = R("mx", 7, 1024, 8)
        act(R("pq"), sp, ACT.Identity, 1.0 / 136.0, 192.0 - 241.0 - 0.4963)
        act(R("tf1"), sp, ACT.Identity, 2.0, -65552.0)
        act(R("tf2"), R("tob"), ACT.Identity, float(CAP - 2))
        act(R("tf3"), sp, ACT.Relu, 16384.0, -16384.0 * (32776.0 + SLOTS - 0.5))
        act(R("tf0"), R("pq"), ACT.Identity, float(1 - CAP), 192.0 * (CAP - 1))
        tt(R("tf1"), R("tf1"), R("tf2"), ALU.add)
        tt(R("tf3"), R("tf3"), R("tf0"), ALU.add)
        tt(R("tf1"), R("tf1"), R("tf3"), ALU.add)
        ts(R("rpu"), R("tf1"), float(SLOTS), ALU.min)
        for k in range(4):
            tt(CR("hrow", k), IND(R("e2"), CL("xu", k)), CR("frow", k), ALU.min)
        idle()
        for k in range(4):
            gat("AV"[k & 1], CR("far", k), R(land), CL("rpu", k), [("rp%d" % t, n_rp)])
            mm([(CR("psv", k), R("id3"), CR("far", k), False, True)])
            either("A", CR("qq", k), CR("psv", k), -127.5)

    def newb(k, dst, base, q="V"):
        if q == "V": return tt(CR(dst, k, base), CR("psv", k), CR("qq", k), ALU.subtract)
        mm([(CR("psv", k), R("cs0"), R("ones"), True, False), (CR("psv", k), R("idb"), CR("old", k), False, False),
            (CR("psv", k), R("id3"), CR("far", k), False, False), (CR("psv", k), R("idn"), CR("qq", k), False, True)])
        return either("A", CR(dst, k, base), CR("psv", k))

    def appended():
        count_start()
        for h in range(2): to_list("zw", "old", h, True, False)
        for k in range(4):
            tt(CR("r0", k), IND(R("rt"), CL("rnu", k)), CR("m1", k), ALU.max)
            tt(CR("wi", k, 2048), IND(R("wi", 0, 2048), CL("inu", k)), CR("hrow", k), ALU.max)
        for h in range(2):
            either("A", HR("frow", h), HR("frow", h), 2048.0)

    exchange(0, appended)

    WOFF = 256.0 * 49152.0

    def SF(h): return R("so", 128 * h + 1, 128 * h + 128, 2)

    def dec(h, tmp, dst, base):
        tt(H(tmp, h), lps(h), SF(h), ALU.min)
        ts(H(dst, h), H(tmp, h), base, ALU.add)

    for k in range(4):
        newb(k, "wb", 4096, "A" if k in OPT["act_new"] else "V")
    for h in range(2):
        to_list("zw3", "far", h, False, False)
        to_list("zwn", "qq", h, False, True)
        ts(H("ti0", h), lps(h), WOFF, ALU.add)
        ts(H("ti4", h), H("ti0", h), 255, ALU.bitwise_and)
        cp(H("xu", h), H("ti4", h))
        ts(H("ti2", h), H("ti0", h), 7, ALU.bitwise_and)
        ts(H("ti3", h), H("ti0", h), 16383, ALU.bitwise_and)
        ts(R("sa", 128 * h + 1, 128 * h + 128, 2), H("ti2", h), 0.0, ALU.is_equal, 0.125, ALU.mult)
        tt(R("sb", 128 * h, 128 * h + 128, 2), H("ti3", h), H("f8a", h), ALU.subtract)
        scan(R("so", 128 * h, 128 * h + 128), R("sa", 128 * h, 128 * h + 128), R("sb", 128 * h, 128 * h + 128), ALU.add)
        cp(H("su", h), SF(h))
        for k in (2 * h, 2 * h + 1):
            gat("A", CR("m1", k), R("e1"), CL("xu", k))
            gat("A", CR("m2", k), R("e2"), CL("xu", k))
            tt(CR("pp", k), IND(R("r0"), CL("su", k)), CR("m1", k), ALU.min)
        to_list("zo", "pp", h, const="cr")
        dec(h, "tf0", "inu", 2048.0)
        for k in (2 * h, 2 * h + 1):
            tt(CR("pp", k), IND(R("wi"), CL("inu", k)), CR("m2", k), ALU.min)
        to_list("zo", "pp", h, const="ci")
        dec(h, "tf4", "bku", 4096.0)
    old_blocks(R("wb", 0, 6144))

    outs = []
    WB = R("psl", 0, 128)

    def blist(z, src, k, start, stop):
        mm([(WB, R(z, 15 - j, 143 - j), R(src, 128 * j, 128 * j + 128), start and j == 0, stop and j == 15) for j in range(4 * k, 4 * k + 4)])

    def inner_out():
        for k in range(4): blist("zw", "old", k, True, False)
        for k in range(4):
            tt(CR("r0", k), IND(R("wi"), CL("inu", k)), CR("hrow", k), ALU.max)
            either("A", CR("r0", k), CR("r0", k), 2048.0)
        for h in range(2):
            lf = "lf%d" % (2 + h)
            outs.append(dma("S", T.yi[:, 1024 * h:1024 * h + 1024], HR("r0", h)[0], [HR("r0", h)], [], [(lf, left[lf])]))

    exchange(1, inner_out)

    for k in range(4):
        blist("zw3", "far", k, False, False)
    for k in range(4):
        blist("zwn", "qq", k, False, True)
        newb(k, "m1", 0)
        outs.append(dma("S", T.yb[:, 512 * k:512 * k + 512], CR("m1", k)[0], [CR("m1", k)], []))
    ts(R("ti0"), WB, WOFF + 256.0, ALU.add)
    ts(R("ti2"), R("ti0"), 7, ALU.bitwise_and)
    ts(R("ti3"), R("ti0"), 16383, ALU.bitwise_and)
    ts(R("tf0"), R("ti2"), 0.0, ALU.is_equal, 0.125, ALU.mult)
    tt(R("tf1"), R("ti3"), R("f8b"), ALU.subtract)
    tt(R("tf1"), R("tf1"), R("tf0"), ALU.mult)
    tt(R("tf2"), R("tf1"), R("fyb"), ALU.add)
    outs.append(dma("A", T.yn[:], T.tf2[:], [R("tf2")], []))
    add("S", [], [], [], sorted(left.items()), False, outs)
    return ops
